import numpy as np
import ml_dtypes


def mxq(x, axis, fmt="e4m3"):
    dtype, down = {"e4m3": (ml_dtypes.float8_e4m3fn, 7), "e5m2": (ml_dtypes.float8_e5m2, 14)}[fmt]
    v = np.moveaxis(np.asarray(x, np.float32).astype(ml_dtypes.bfloat16).astype(np.float64), axis, -1)
    blocks = v.reshape(v.shape[:-1] + (-1, 32))
    amax = np.abs(blocks).max(-1, keepdims=True)
    byte = np.maximum(np.where(amax > 0, np.frexp(amax)[1] - 1 + 127, 0) - down, 1)
    scale = np.exp2(byte - 127.0)
    codes = (blocks / scale).astype(np.float32).astype(dtype).astype(np.float64)
    return np.moveaxis((codes * scale).reshape(v.shape), -1, axis)


WIDE = False


def mx_kscale(k):
    if not WIDE:
        return np.ones(k)
    levels = np.array([10, -10, 5, -5, 0])
    if k % 512:
        return np.exp2(np.random.permutation(np.resize(levels, k // 32))).repeat(32)
    a = np.empty((k // 512, 16))
    for p in range(k // 512):
        a[p, :8] = np.random.permutation(np.resize(levels, 8))
        for g in range(8):
            far = levels[np.abs(levels - a[p, g]) >= 10]
            a[p, g + 8] = far[np.random.randint(len(far))]
    return np.exp2(a.ravel()).repeat(32)


def f64(x):
    return np.asarray(x).astype(np.float64)


def striped(idx):
    return np.tile(idx.reshape(-1, 16).T, (8, 1)).astype(np.uint16)


def unstriped(offs):
    return offs[:16].T.reshape(-1).astype(np.int64)


E2M1 = np.array([0.0, 0.5, 1.0, 1.5, 2.0, 3.0, 4.0, 6.0, -0.0, -0.5, -1.0, -1.5, -2.0, -3.0, -4.0, -6.0])


def pack_weight(w, fmt):
    k, n = w.shape
    w = f64(np.asarray(w, np.float32).astype(ml_dtypes.bfloat16)).reshape(k // 32, 32, n)
    amax = np.abs(w).max(1)
    if fmt == "e4m3":
        byte = np.frexp(amax)[1] - 1 + 127 - 7
    else:
        mant, ex = np.frexp(amax / 6.0)
        byte = np.where(mant > 0.5, ex, ex - 1) + 127
    byte = np.clip(np.where(amax > 0, byte, 1), 1, 254)
    scaled = (w * np.exp2(127.0 - byte)[:, None, :]).reshape(k, n).astype(np.float32)
    by_word = np.ascontiguousarray(scaled.reshape(k // 512, 128, 4, n).transpose(0, 1, 3, 2))
    if fmt == "e4m3":
        words = by_word.astype(ml_dtypes.float8_e4m3fn).view(np.uint8)
    else:
        c = by_word.astype(ml_dtypes.float4_e2m1fn).view(np.uint8) & 0xF
        words = (c[..., 0::2] | (c[..., 1::2] << 4)).reshape(k // 512, 128, 2 * n)
    return np.ascontiguousarray(words), np.ascontiguousarray(byte.astype(np.uint8).reshape(k // 512, 16, n))


def unpack_weight(words, scales, fmt):
    g, _, n = scales.shape
    words = np.ascontiguousarray(words).reshape(g, 128, n, -1)
    if fmt == "e4m3":
        vals = words.view(ml_dtypes.float8_e4m3fn).astype(np.float64)
    else:
        nib = np.empty((g, 128, n, 4), np.uint8)
        nib[..., 0::2] = words & 0xF
        nib[..., 1::2] = words >> 4
        vals = E2M1[nib]
    vals = vals * np.repeat(np.exp2(scales.astype(np.float64) - 127.0), 8, axis=1)[..., None]
    return vals.transpose(0, 1, 3, 2).reshape(g * 512, n)


def gelu(v):
    return 0.5 * v * (1.0 + np.tanh(np.sqrt(2.0 / np.pi) * (v + 0.044715 * v**3)))


K, T, S, H, P = 1536, 4096, 1024, 1024, 512


def setup_inputs():
    n = np.random.standard_normal
    s = mx_kscale(K)[:, None]
    u = mx_kscale(H)[:, None]
    tab_words, tab_scales = pack_weight(n((K, T)) * s, "e4m3")
    w1_words, w1_scales = pack_weight(n((K, H)) / np.sqrt(K) / s, "e2m1")
    return {
        "tab_words": tab_words,
        "tab_scales": tab_scales,
        "offs": striped(np.random.permutation(T)[:S]),
        "pos1": striped(np.random.permutation(S)[:P]),
        "w1_words": w1_words,
        "w1_scales": w1_scales,
        "fog": (0.8 * n((H, S))).astype(np.float32),
        "gain": (np.exp(0.3 * n(H)) * u[:, 0]).astype(np.float32),
        "w2": (1.8 * n((H, H)) / np.sqrt(H) / u).astype(np.float32),
        "mend": np.exp(0.3 * n(H)).astype(np.float32),
        "skip": (np.exp(0.3 * n(H)) / u[:, 0]).astype(np.float32),
        "wgo": np.exp(0.3 * n((128, P))).astype(np.float32),
    }


def reference(tab_words, tab_scales, offs, pos1, w1_words, w1_scales, fog, gain, w2, mend, skip, wgo):
    v = unpack_weight(tab_words, tab_scales, "e4m3")[:, unstriped(offs)]
    w1 = unpack_weight(w1_words, w1_scales, "e2m1")
    h = f64(gain)[:, None] * np.tanh((w1.T @ v) + f64(fog))
    x = mxq(h[:, unstriped(pos1)], 0, "e4m3")
    w2q = mxq(f64(w2), 0, "e4m3")
    y = f64(mend)[:, None] * np.tanh(w2q.T @ x)
    out = f64(skip)[:, None] * h + f64(fog)
    out[:, unstriped(pos1)] = np.tile(f64(wgo), (H // 128, 1)) * y
    return out

@@ -1,0 +1,254 @@
+from contextlib import ExitStack
+
+import concourse.mybir as mybir
+
+K, T, S, H, PICK = 1536, 4096, 1024, 1024, 512
+FLOPS = 2 * K * H * S + 2 * H * H * PICK
+
+F32 = mybir.dt.float32
+BF16 = mybir.dt.bfloat16
+I32 = mybir.dt.int32
+U32 = mybir.dt.uint32
+U16 = mybir.dt.uint16
+U8 = mybir.dt.uint8
+FP8X4 = mybir.dt.float8_e4m3fn_x4
+FP4X4 = mybir.dt.float4_e2m1fn_x4
+MULT = mybir.AluOpType.mult
+ADD = mybir.AluOpType.add
+TANH = mybir.ActivationFunctionType.Tanh
+COPY = mybir.ActivationFunctionType.Copy
+
+P = 128
+PACK = 4
+K_PASS = P * PACK
+BANK = 512
+PASSES1 = K // K_PASS
+PASSES2 = H // K_PASS
+SLICES = H // P
+HALVES = S // BANK
+BANKS = 8
+SHIFT_ROWS = 112
+
+
+def tile_list_plate_scratch_restorer_kernel(
+    tc, tab_words, tab_scales, offs, pos1, w1_words, w1_scales, fog, gain, w2, mend, skip, wgo, out
+):
+    nc = tc.nc
+    with ExitStack() as ctx:
+        lists = ctx.enter_context(tc.tile_pool(name="lists", bufs=1))
+        keep = ctx.enter_context(tc.tile_pool(name="keep", bufs=1))
+        ring = ctx.enter_context(tc.tile_pool(name="ring", bufs=3))
+        psum = ctx.enter_context(tc.psum_pool(name="psum", bufs=BANKS))
+
+        idx = lists.tile([P, S // 16], U16, name="idx")
+        picks = lists.tile([P, PICK // 16], U16, name="picks")
+        nc.sync.dma_start(idx[:], offs)
+
+        tab_sc = keep.tile([P, T], U8, name="tab_sc", tag="tab_sc", align_bytes=64)
+        w1_sc_raw = keep.tile([P, PASSES1 * H], U8, name="w1_sc_raw", tag="w1_sc_raw", align_bytes=64)
+        v_sc = [keep.tile([P, S], U8, name="v_sc%d" % a, align_bytes=64) for a in range(PASSES1)]
+        nc.gpsimd.memset(tab_sc[:].bitcast(I32), 0)
+        nc.vector.memset(w1_sc_raw[:].bitcast(I32), 0)
+        for a in range(1, PASSES1):
+            nc.vector.memset(v_sc[a][96:P, :].bitcast(I32), 0)
+
+        w1_raw = keep.tile([P, PASSES1 * 2 * H], U8, name="w1_raw", align_bytes=64)
+        nc.sync.dma_start(
+            out=w1_raw[:].bitcast(I32).rearrange("p (a c) -> p a c", a=PASSES1),
+            in_=w1_words.bitcast(I32).rearrange("a p c -> p a c"),
+        )
+        tab = [keep.tile([P, T], U32, name="tab%d" % a, tag="tab%d" % a, align_bytes=64) for a in range(PASSES1)]
+
+        def load_tab(a):
+            nc.sync.dma_start(
+                out=tab[a][:].bitcast(I32),
+                in_=tab_words[a].rearrange("p t i -> p (t i)").bitcast(I32),
+            )
+
+        for a in range(PASSES1):
+            load_tab(a)
+        nc.sync.dma_start(picks[:], pos1)
+        gain_t = keep.tile([P, PASSES2, PACK], F32, name="gain_t")
+        skip_t = keep.tile([P, PASSES2, PACK], F32, name="skip_t")
+        mend_t = keep.tile([P, PASSES2, PACK], F32, name="mend_t")
+        for dst, src in ((gain_t, gain), (skip_t, skip), (mend_t, mend)):
+            nc.scalar.dma_start(out=dst[:], in_=src.rearrange("(b p t) -> p b t", p=P, t=PACK))
+        for q in range(4):
+            nc.gpsimd.dma_start(
+                out=tab_sc[32 * q : 32 * q + 4 * PASSES1, :].bitcast(I32),
+                in_=tab_scales[:, 4 * q : 4 * q + 4, :].bitcast(I32),
+            )
+        for q in range(4):
+            nc.gpsimd.dma_start(
+                out=w1_sc_raw[32 * q : 32 * q + 4, :].bitcast(I32).rearrange("r (a c) -> r a c", a=PASSES1),
+                in_=w1_scales[:, 4 * q : 4 * q + 4, :].bitcast(I32).rearrange("a r c -> r a c"),
+            )
+
+        fog_rows = fog.rearrange("(b p t) j -> b t p j", p=P, t=PACK)
+        out_rows = out.rearrange("(b p t) j -> b t p j", p=P, t=PACK)
+        page = [keep.tile([P, S], F32, name="page%d" % s) for s in range(SLICES)]
+        w2_raw = [
+            keep.tile([P, PASSES2, PACK, BANK], F32, name="w2_raw%d" % c, tag=("w2_raw", "tab2")[c], align_bytes=64)
+            for c in range(2)
+        ]
+        wgo_t = keep.tile([P, PACK * PICK], F32, name="wgo_t")
+
+        def load_fog(s):
+            nc.sync.dma_start(out=page[s][:], in_=fog_rows[s // PACK][s % PACK])
+
+        def load_w2(b, c):
+            nc.sync.dma_start(
+                out=w2_raw[c][:, b],
+                in_=w2[b * K_PASS : (b + 1) * K_PASS, c * K_PASS : (c + 1) * K_PASS].rearrange("(p j) n -> p j n", j=PACK),
+            )
+
+        load_fog(0)
+        load_fog(1)
+        load_w2(0, 0)
+        load_fog(2)
+        load_fog(3)
+        load_w2(1, 0)
+        for s in range(4, SLICES):
+            load_fog(s)
+        for u in range(4):
+            nc.sync.dma_start(out=wgo_t[32 * u : 32 * u + 32, :], in_=wgo.rearrange("(q t) m -> q (t m)", t=PACK))
+        load_w2(0, 1)
+        load_w2(1, 1)
+
+        w1_codes = keep.tile([P, PASSES1 * 2 * H], U8, name="w1_codes", align_bytes=64)
+        w1_sc = keep.tile([P, PASSES1 * H], U8, name="w1_sc", align_bytes=64)
+        nc.vector.tensor_copy(
+            out=w1_codes[:].bitcast(U16).rearrange("p (g t q) -> p g t q", t=PACK, q=P),
+            in_=w1_raw[:].bitcast(U16).rearrange("p (g q t) -> p g t q", t=PACK, q=P),
+        )
+        nc.vector.tensor_copy(
+            out=w1_sc[:].rearrange("p (g t q) -> p g t q", t=PACK, q=P),
+            in_=w1_sc_raw[:].rearrange("p (g q t) -> p g t q", t=PACK, q=P),
+        )
+
+        nc.vector.tensor_copy(out=v_sc[0][:], in_=tab_sc[:].indirect(idx[:]))
+        for a in range(1, PASSES1):
+            nc.gpsimd.dma_start(
+                out=v_sc[a][0:SHIFT_ROWS, :].bitcast(I32),
+                in_=v_sc[0][4 * a : 4 * a + SHIFT_ROWS, :].bitcast(I32),
+            )
+        v0 = keep.tile([P, S], U32, name="v0", tag="tab_sc", align_bytes=64)
+        v1a = keep.tile([P, BANK], U32, name="v1a", tag="tab0", align_bytes=64)
+        v1b = keep.tile([P, BANK], U32, name="v1b", tag="w1_sc_raw", align_bytes=64)
+        v2 = keep.tile([P, S], U32, name="v2", tag="tab1", align_bytes=64)
+        v_codes = [[v0[:, :BANK], v0[:, BANK:]], [v1a[:], v1b[:]], [v2[:, :BANK], v2[:, BANK:]]]
+        cols = BANK // 16
+        for a in range(PASSES1):
+            for h in range(HALVES):
+                nc.vector.tensor_copy(out=v_codes[a][h], in_=tab[a][:].indirect(idx[:, h * cols : (h + 1) * cols]))
+
+
+        def first_pass(acc, s, h, a):
+            col = a * H + s * P
+            nc.tensor.matmul_mx(
+                out=acc[:],
+                lhsT=w1_codes[:, 2 * col : 2 * (col + P)].bitcast(FP4X4),
+                lhsT_scale=w1_sc[:, col : col + P],
+                rhs=v_codes[a][h].bitcast(FP8X4),
+                rhs_scale=v_sc[a][:, h * BANK : (h + 1) * BANK],
+                start=(a == 0),
+                stop=(a == PASSES1 - 1),
+            )
+
+        feat = [keep.tile([P, S], F32, name="feat%d" % s) for s in range(SLICES)]
+        x_codes = [keep.tile([P, PICK], U32, name="x_codes%d" % b, align_bytes=64) for b in range(PASSES2)]
+        x_sc = [keep.tile([P, PICK], U8, name="x_sc%d" % b, align_bytes=64) for b in range(PASSES2)]
+        w2_codes = {}
+        w2_sc = {}
+        for b in range(PASSES2):
+            for c in range(2):
+                w2_codes[b, c] = keep.tile([P, K_PASS], U32, name="w2_codes%d%d" % (b, c), align_bytes=64)
+                w2_sc[b, c] = keep.tile([P, K_PASS], U8, name="w2_sc%d%d" % (b, c), align_bytes=64)
+
+        def quantise_w2(b, c):
+            grouped = ring.tile([P, PACK * K_PASS], BF16, name="w2_grouped", bufs=2, align_bytes=64)
+            nc.scalar.copy(
+                out=grouped[:].rearrange("p (t q j) -> p q t j", t=PACK, j=PACK),
+                in_=w2_raw[c][:, b].rearrange("p j (q t) -> p q t j", t=PACK),
+            )
+            nc.vector.quantize_mx(out=w2_codes[b, c][:].bitcast(FP8X4), scales=w2_sc[b, c][:], in_=grouped[:])
+
+        early = BANKS // HALVES
+        accs = {}
+        for s in range(early):
+            for h in range(HALVES):
+                accs[s, h] = psum.tile([P, BANK], F32, name="acc", tag="acc")
+        for a in range(PASSES1):
+            for h in range(HALVES):
+                for s in range(early):
+                    first_pass(accs[s, h], s, h, a)
+
+        rounded = [ring.tile([P, PACK, PICK], BF16, name="rounded%d" % b, bufs=1) for b in range(PASSES2)]
+
+        def features(s):
+            for h in range(HALVES):
+                if s >= early:
+                    accs[s, h] = psum.tile([P, BANK], F32, name="acc", tag="acc")
+                    for a in range(PASSES1):
+                        first_pass(accs[s, h], s, h, a)
+                half = slice(h * BANK, (h + 1) * BANK)
+                nc.vector.tensor_tensor(out=feat[s][:, half], in0=accs[s, h][:], in1=page[s][:, half], op=ADD)
+            nc.scalar.activation(out=feat[s][:], in_=feat[s][:], func=TANH)
+
+        def pick(s):
+            b, t = divmod(s, PACK)
+            picked = ring.tile([P, PICK], F32, name="picked")
+            nc.vector.tensor_copy(out=picked[:], in_=feat[s][:].indirect(picks[:]))
+            nc.scalar.activation(out=rounded[b][:, t, :], in_=picked[:], func=COPY, scale=gain_t[:, b, t : t + 1])
+
+        def quantise_x(b):
+            woven = ring.tile([P, PICK * PACK], BF16, name="woven", bufs=2, align_bytes=64)
+            nc.vector.tensor_copy(
+                out=woven[:].rearrange("p (c i t) -> p c t i", i=4, t=PACK),
+                in_=rounded[b][:].rearrange("p t (c i) -> p c t i", i=4),
+            )
+            nc.vector.quantize_mx(out=x_codes[b][:].bitcast(FP8X4), scales=x_sc[b][:], in_=woven[:])
+
+        features(0)
+        for s in range(SLICES):
+            if s + 1 < SLICES:
+                features(s + 1)
+            pick(s)
+            if s == 2:
+                quantise_w2(0, 0)
+            if s == 4:
+                quantise_x(0)
+            if s == 5:
+                quantise_w2(1, 0)
+        quantise_x(1)
+        gs_t = keep.tile([P, PASSES2, PACK], F32, name="gs_t", tag="tab1", align_bytes=64)
+        nc.vector.tensor_tensor(out=gs_t[:], in0=gain_t[:], in1=skip_t[:], op=MULT)
+
+        for s in range(SLICES):
+            c, t = divmod(s, PACK)
+            if s == 1:
+                quantise_w2(0, 1)
+            if s == 2:
+                quantise_w2(1, 1)
+            acc = psum.tile([P, PICK], F32, name="acc", tag="acc")
+            for b in range(PASSES2):
+                nc.tensor.matmul_mx(
+                    out=acc[:],
+                    lhsT=w2_codes[b, c][:, t * P : (t + 1) * P].bitcast(FP8X4),
+                    lhsT_scale=w2_sc[b, c][:, t * P : (t + 1) * P],
+                    rhs=x_codes[b][:].bitcast(FP8X4),
+                    rhs_scale=x_sc[b][:],
+                    start=(b == 0),
+                    stop=(b == PASSES2 - 1),
+                )
+            weight = ring.tile([P, PICK], F32, name="weight")
+            nc.scalar.activation(
+                out=weight[:], in_=wgo_t[:, t * PICK : (t + 1) * PICK], func=COPY, scale=mend_t[:, c, t : t + 1]
+            )
+            mended = ring.tile([P, PICK], F32, name="mended")
+            nc.scalar.activation(out=mended[:], in_=acc[:], func=TANH)
+            nc.vector.scalar_tensor_tensor(
+                out=page[s][:], in0=feat[s][:], scalar=gs_t[:, c, t : t + 1], in1=page[s][:], op0=MULT, op1=ADD
+            )
+            nc.vector.tensor_tensor(out=page[s][:].indirect(picks[:]), in0=mended[:], in1=weight[:], op=MULT)
+            nc.sync.dma_start(out=out_rows[c][t], in_=page[s][:])

@@ -27,7 +27,7 @@ PASSES2 = H // K_PASS
 SLICES = H // P
 HALVES = S // BANK
 BANKS = 8
-SHIFT_ROWS = 112
+FIRST_ROW = P - 16 * PASSES1
 
 
 def tile_list_plate_scratch_restorer_kernel(
@@ -37,120 +37,119 @@ def tile_list_plate_scratch_restorer_kernel(
     with ExitStack() as ctx:
         lists = ctx.enter_context(tc.tile_pool(name="lists", bufs=1))
         keep = ctx.enter_context(tc.tile_pool(name="keep", bufs=1))
+        shared = ctx.enter_context(tc.tile_pool(name="shared", bufs=1))
         ring = ctx.enter_context(tc.tile_pool(name="ring", bufs=3))
         psum = ctx.enter_context(tc.psum_pool(name="psum", bufs=BANKS))
 
         idx = lists.tile([P, S // 16], U16, name="idx")
         picks = lists.tile([P, PICK // 16], U16, name="picks")
         nc.sync.dma_start(idx[:], offs)
+        nc.sync.dma_start(picks[:], pos1)
 
-        tab_sc = keep.tile([P, T], U8, name="tab_sc", tag="tab_sc", align_bytes=64)
-        w1_sc_raw = keep.tile([P, PASSES1 * H], U8, name="w1_sc_raw", tag="w1_sc_raw", align_bytes=64)
-        v_sc = [keep.tile([P, S], U8, name="v_sc%d" % a, align_bytes=64) for a in range(PASSES1)]
-        nc.gpsimd.memset(tab_sc[:].bitcast(I32), 0)
-        nc.vector.memset(w1_sc_raw[:].bitcast(I32), 0)
-        for a in range(1, PASSES1):
-            nc.vector.memset(v_sc[a][96:P, :].bitcast(I32), 0)
+        def placed(name, shape, dtype, kib):
+            return shared.tile(shape, dtype, name=name, offset=kib * 1024, align_bytes=64)
 
-        w1_raw = keep.tile([P, PASSES1 * 2 * H], U8, name="w1_raw", align_bytes=64)
+        tab = [placed("tab%d" % a, [P, T], U32, 16 * a) for a in range(PASSES1)]
+        tab_sc = placed("tab_sc", [P, T], U8, 58)
+        w1_codes = placed("w1_codes", [P, PASSES1 * 2 * H], U8, 48)
+        w1_raw = placed("w1_raw", [P, PASSES1 * 2 * H], U8, 66)
+        v_sc_rows = shared.tile([P, S], U8, name="v_sc_rows", offset=48 * 1024 - S // 2, align_bytes=64)
+        page = [placed("page%d" % s, [P, S], F32, (0, 4, 16, 20, 32, 36, 40, 44)[s]) for s in range(SLICES)]
+        w2_raw = {}
+        for b, c, kib in ((0, 0, 8), (1, 0, 24), (0, 1, 24), (1, 1, 54)):
+            w2_raw[b, c] = placed("w2_raw%d%d" % (b, c), [P, PACK, BANK], F32, kib)
+        wgo_t = placed("wgo_t", [P, PACK * PICK], F32, 8)
+        v_codes = [placed("v%d" % a, [P, S], U32, 54 + 4 * a) for a in range(PASSES1)]
+        gs_t = placed("gs_t", [P, PASSES2, PACK], F32, 62)
+
+        w1_sc_raw = keep.tile([P, H], U8, name="w1_sc_raw", align_bytes=64)
+        rows_both = keep.tile([P, H + S], U8, name="rows_both", align_bytes=64)
+        gain_t = shared.tile([P, PASSES2, PACK], F32, name="gain_t", offset=66 * 1024, align_bytes=64)
+        skip_t = shared.tile([P, PASSES2, PACK], F32, name="skip_t", offset=66 * 1024 + 64, align_bytes=64)
+        mend_t = shared.tile([P, PASSES2, PACK], F32, name="mend_t", offset=66 * 1024 + 128, align_bytes=64)
+        planes = keep.tile([P, PASSES1 * (H + S)], U8, name="planes", align_bytes=64)
         nc.sync.dma_start(
             out=w1_raw[:].bitcast(I32).rearrange("p (a c) -> p a c", a=PASSES1),
             in_=w1_words.bitcast(I32).rearrange("a p c -> p a c"),
         )
-        tab = [keep.tile([P, T], U32, name="tab%d" % a, tag="tab%d" % a, align_bytes=64) for a in range(PASSES1)]
+        for rows, scales in ((w1_sc_raw, w1_scales), (tab_sc, tab_scales)):
+            nc.sync.dma_start(
+                out=rows[FIRST_ROW:P, :].bitcast(I32), in_=scales.bitcast(I32).rearrange("a q c -> q a c")
+            )
+            nc.vector.memset(rows[0:64, :].bitcast(I32), 0)
+            nc.vector.memset(rows[64:FIRST_ROW, :].bitcast(I32), 0)
+        nc.vector.memset(planes[:].bitcast(I32), 0)
 
         def load_tab(a):
             nc.sync.dma_start(
-                out=tab[a][:].bitcast(I32),
-                in_=tab_words[a].rearrange("p t i -> p (t i)").bitcast(I32),
+                out=tab[a][:].bitcast(I32), in_=tab_words[a].rearrange("p t i -> p (t i)").bitcast(I32)
             )
 
-        for a in range(PASSES1):
-            load_tab(a)
-        nc.sync.dma_start(picks[:], pos1)
-        gain_t = keep.tile([P, PASSES2, PACK], F32, name="gain_t")
-        skip_t = keep.tile([P, PASSES2, PACK], F32, name="skip_t")
-        mend_t = keep.tile([P, PASSES2, PACK], F32, name="mend_t")
+        load_tab(0)
+        load_tab(1)
+        nc.vector.tensor_copy(
+            out=rows_both[:, :H].rearrange("p (g t q) -> p g t q", t=PACK, q=P),
+            in_=w1_sc_raw[:].rearrange("p (g q t) -> p g t q", t=PACK, q=P),
+        )
+        nc.vector.tensor_copy(out=v_sc_rows[:], in_=tab_sc[:].indirect(idx[:]))
+        nc.vector.tensor_copy(out=rows_both[:, H:].bitcast(I32), in_=v_sc_rows[:].bitcast(I32))
+        for q in range(4):
+            first = FIRST_ROW + 4 * PASSES1 * q
+            (nc.scalar, nc.sync)[q % 2].dma_start(
+                out=planes[32 * q : 32 * q + 4, :].bitcast(I32).rearrange("r (a c) -> r a c", a=PASSES1),
+                in_=rows_both[first : first + 4 * PASSES1, :].bitcast(I32),
+            )
+        load_tab(2)
         for dst, src in ((gain_t, gain), (skip_t, skip), (mend_t, mend)):
             nc.scalar.dma_start(out=dst[:], in_=src.rearrange("(b p t) -> p b t", p=P, t=PACK))
-        for q in range(4):
-            nc.gpsimd.dma_start(
-                out=tab_sc[32 * q : 32 * q + 4 * PASSES1, :].bitcast(I32),
-                in_=tab_scales[:, 4 * q : 4 * q + 4, :].bitcast(I32),
-            )
-        for q in range(4):
-            nc.gpsimd.dma_start(
-                out=w1_sc_raw[32 * q : 32 * q + 4, :].bitcast(I32).rearrange("r (a c) -> r a c", a=PASSES1),
-                in_=w1_scales[:, 4 * q : 4 * q + 4, :].bitcast(I32).rearrange("a r c -> r a c"),
-            )
 
         fog_rows = fog.rearrange("(b p t) j -> b t p j", p=P, t=PACK)
         out_rows = out.rearrange("(b p t) j -> b t p j", p=P, t=PACK)
-        page = [keep.tile([P, S], F32, name="page%d" % s) for s in range(SLICES)]
-        w2_raw = [
-            keep.tile([P, PASSES2, PACK, BANK], F32, name="w2_raw%d" % c, tag=("w2_raw", "tab2")[c], align_bytes=64)
-            for c in range(2)
-        ]
-        wgo_t = keep.tile([P, PACK * PICK], F32, name="wgo_t")
 
         def load_fog(s):
             nc.sync.dma_start(out=page[s][:], in_=fog_rows[s // PACK][s % PACK])
 
         def load_w2(b, c):
             nc.sync.dma_start(
-                out=w2_raw[c][:, b],
+                out=w2_raw[b, c][:],
                 in_=w2[b * K_PASS : (b + 1) * K_PASS, c * K_PASS : (c + 1) * K_PASS].rearrange("(p j) n -> p j n", j=PACK),
             )
 
-        load_fog(0)
-        load_fog(1)
-        load_w2(0, 0)
-        load_fog(2)
-        load_fog(3)
-        load_w2(1, 0)
-        for s in range(4, SLICES):
-            load_fog(s)
-        for u in range(4):
-            nc.sync.dma_start(out=wgo_t[32 * u : 32 * u + 32, :], in_=wgo.rearrange("(q t) m -> q (t m)", t=PACK))
-        load_w2(0, 1)
-        load_w2(1, 1)
-
-        w1_codes = keep.tile([P, PASSES1 * 2 * H], U8, name="w1_codes", align_bytes=64)
-        w1_sc = keep.tile([P, PASSES1 * H], U8, name="w1_sc", align_bytes=64)
         nc.vector.tensor_copy(
             out=w1_codes[:].bitcast(U16).rearrange("p (g t q) -> p g t q", t=PACK, q=P),
             in_=w1_raw[:].bitcast(U16).rearrange("p (g q t) -> p g t q", t=PACK, q=P),
         )
-        nc.vector.tensor_copy(
-            out=w1_sc[:].rearrange("p (g t q) -> p g t q", t=PACK, q=P),
-            in_=w1_sc_raw[:].rearrange("p (g q t) -> p g t q", t=PACK, q=P),
-        )
 
-        nc.vector.tensor_copy(out=v_sc[0][:], in_=tab_sc[:].indirect(idx[:]))
-        for a in range(1, PASSES1):
-            nc.gpsimd.dma_start(
-                out=v_sc[a][0:SHIFT_ROWS, :].bitcast(I32),
-                in_=v_sc[0][4 * a : 4 * a + SHIFT_ROWS, :].bitcast(I32),
-            )
-        v0 = keep.tile([P, S], U32, name="v0", tag="tab_sc", align_bytes=64)
-        v1a = keep.tile([P, BANK], U32, name="v1a", tag="tab0", align_bytes=64)
-        v1b = keep.tile([P, BANK], U32, name="v1b", tag="w1_sc_raw", align_bytes=64)
-        v2 = keep.tile([P, S], U32, name="v2", tag="tab1", align_bytes=64)
-        v_codes = [[v0[:, :BANK], v0[:, BANK:]], [v1a[:], v1b[:]], [v2[:, :BANK], v2[:, BANK:]]]
         cols = BANK // 16
-        for a in range(PASSES1):
-            for h in range(HALVES):
-                nc.vector.tensor_copy(out=v_codes[a][h], in_=tab[a][:].indirect(idx[:, h * cols : (h + 1) * cols]))
 
+        def gather_words(a):
+            for h in range(HALVES):
+                nc.vector.tensor_copy(
+                    out=v_codes[a][:, h * BANK : (h + 1) * BANK],
+                    in_=tab[a][:].indirect(idx[:, h * cols : (h + 1) * cols]),
+                )
+
+        gather_words(0)
+        load_fog(0)
+        load_fog(1)
+        load_w2(0, 0)
+        gather_words(1)
+        load_fog(2)
+        load_fog(3)
+        load_w2(1, 0)
+        gather_words(2)
+        for s in range(4, SLICES):
+            load_fog(s)
 
         def first_pass(acc, s, h, a):
             col = a * H + s * P
+            plane = a * (H + S)
             nc.tensor.matmul_mx(
                 out=acc[:],
                 lhsT=w1_codes[:, 2 * col : 2 * (col + P)].bitcast(FP4X4),
-                lhsT_scale=w1_sc[:, col : col + P],
-                rhs=v_codes[a][h].bitcast(FP8X4),
-                rhs_scale=v_sc[a][:, h * BANK : (h + 1) * BANK],
+                lhsT_scale=planes[:, plane + s * P : plane + (s + 1) * P],
+                rhs=v_codes[a][:, h * BANK : (h + 1) * BANK].bitcast(FP8X4),
+                rhs_scale=planes[:, plane + H + h * BANK : plane + H + (h + 1) * BANK],
                 start=(a == 0),
                 stop=(a == PASSES1 - 1),
             )
@@ -169,7 +168,7 @@ def tile_list_plate_scratch_restorer_kernel(
             grouped = ring.tile([P, PACK * K_PASS], BF16, name="w2_grouped", bufs=2, align_bytes=64)
             nc.scalar.copy(
                 out=grouped[:].rearrange("p (t q j) -> p q t j", t=PACK, j=PACK),
-                in_=w2_raw[c][:, b].rearrange("p j (q t) -> p q t j", t=PACK),
+                in_=w2_raw[b, c][:].rearrange("p j (q t) -> p q t j", t=PACK),
             )
             nc.vector.quantize_mx(out=w2_codes[b, c][:].bitcast(FP8X4), scales=w2_sc[b, c][:], in_=grouped[:])
 
@@ -216,12 +215,17 @@ def tile_list_plate_scratch_restorer_kernel(
             pick(s)
             if s == 2:
                 quantise_w2(0, 0)
+                for u in range(4):
+                    nc.sync.dma_start(
+                        out=wgo_t[32 * u : 32 * u + 32, :], in_=wgo.rearrange("(q t) m -> q (t m)", t=PACK)
+                    )
             if s == 4:
                 quantise_x(0)
             if s == 5:
                 quantise_w2(1, 0)
+                load_w2(0, 1)
         quantise_x(1)
-        gs_t = keep.tile([P, PASSES2, PACK], F32, name="gs_t", tag="tab1", align_bytes=64)
+        load_w2(1, 1)
         nc.vector.tensor_tensor(out=gs_t[:], in0=gain_t[:], in1=skip_t[:], op=MULT)
 
         for s in range(SLICES):

@@ -22,12 +22,23 @@ P = 128
 PACK = 4
 K_PASS = P * PACK
 BANK = 512
+BANKS = 8
+QUADRANTS = 4
+QUADRANT = P // QUADRANTS
+PLANE_ROWS = 4
+LIST_ROWS = 16
 PASSES1 = K // K_PASS
 PASSES2 = H // K_PASS
 SLICES = H // P
 HALVES = S // BANK
-BANKS = 8
-FIRST_ROW = P - 16 * PASSES1
+W2_HALVES = H // K_PASS
+RING = 3
+
+FIRST_ROW = P - QUADRANTS * PLANE_ROWS * PASSES1
+
+TAB_BYTES = 4 * T
+PAGE_BYTES = 4 * S
+ALIGN = 64
 
 
 def tile_list_plate_scratch_restorer_kernel(
@@ -38,36 +49,44 @@ def tile_list_plate_scratch_restorer_kernel(
         lists = ctx.enter_context(tc.tile_pool(name="lists", bufs=1))
         keep = ctx.enter_context(tc.tile_pool(name="keep", bufs=1))
         shared = ctx.enter_context(tc.tile_pool(name="shared", bufs=1))
-        ring = ctx.enter_context(tc.tile_pool(name="ring", bufs=3))
+        ring = ctx.enter_context(tc.tile_pool(name="ring", bufs=RING))
         psum = ctx.enter_context(tc.psum_pool(name="psum", bufs=BANKS))
 
-        idx = lists.tile([P, S // 16], U16, name="idx")
-        picks = lists.tile([P, PICK // 16], U16, name="picks")
+        idx = lists.tile([P, S // LIST_ROWS], U16, name="idx")
+        picks = lists.tile([P, PICK // LIST_ROWS], U16, name="picks")
         nc.sync.dma_start(idx[:], offs)
         nc.sync.dma_start(picks[:], pos1)
 
-        def placed(name, shape, dtype, kib):
-            return shared.tile(shape, dtype, name=name, offset=kib * 1024, align_bytes=64)
+        tab_at = [a * TAB_BYTES for a in range(PASSES1)]
+        page_at = [tab_at[a] + i * PAGE_BYTES for a, count in enumerate((2, 2, 4)) for i in range(count)]
+        piece_at = [tab_at[a] + 2 * PAGE_BYTES for a in range(PASSES2)]
+        w1_codes_at = PASSES1 * TAB_BYTES
+        v_codes_at = [w1_codes_at + PASSES1 * 2 * H + a * PAGE_BYTES for a in range(PASSES1)]
+        rows_at = v_codes_at[-1] + PAGE_BYTES
 
-        tab = [placed("tab%d" % a, [P, T], U32, 16 * a) for a in range(PASSES1)]
-        tab_sc = placed("tab_sc", [P, T], U8, 58)
-        w1_codes = placed("w1_codes", [P, PASSES1 * 2 * H], U8, 48)
-        w1_raw = placed("w1_raw", [P, PASSES1 * 2 * H], U8, 66)
-        v_sc_rows = shared.tile([P, S], U8, name="v_sc_rows", offset=48 * 1024 - S // 2, align_bytes=64)
-        page = [placed("page%d" % s, [P, S], F32, (0, 4, 16, 20, 32, 36, 40, 44)[s]) for s in range(SLICES)]
+        def placed(name, shape, dtype, at):
+            return shared.tile(shape, dtype, name=name, offset=at, align_bytes=ALIGN)
+
+        tab = [placed("tab%d" % a, [P, T], U32, tab_at[a]) for a in range(PASSES1)]
+        tab_sc = placed("tab_sc", [P, T], U8, v_codes_at[1])
+        w1_codes = placed("w1_codes", [P, PASSES1 * 2 * H], U8, w1_codes_at)
+        w1_raw = keep.tile([P, PASSES1 * 2 * H], U8, name="w1_raw", align_bytes=ALIGN)
+        v_sc_rows = placed("v_sc_rows", [P, S], U8, w1_codes_at - S // 2)
+        page = [placed("page%d" % s, [P, S], F32, page_at[s]) for s in range(SLICES)]
         w2_raw = {}
-        for b, c, kib in ((0, 0, 8), (1, 0, 24), (0, 1, 24), (1, 1, 54)):
-            w2_raw[b, c] = placed("w2_raw%d%d" % (b, c), [P, PACK, BANK], F32, kib)
-        wgo_t = placed("wgo_t", [P, PACK * PICK], F32, 8)
-        v_codes = [placed("v%d" % a, [P, S], U32, 54 + 4 * a) for a in range(PASSES1)]
-        gs_t = placed("gs_t", [P, PASSES2, PACK], F32, 62)
+        for b, c, at in ((0, 0, piece_at[0]), (1, 0, piece_at[1]), (0, 1, piece_at[1]), (1, 1, v_codes_at[0])):
+            w2_raw[b, c] = placed("w2_raw%d%d" % (b, c), [P, PACK, K_PASS], F32, at)
+        wgo_dealt = placed("wgo_dealt", [P, PACK * PICK], F32, piece_at[0])
+        v_codes = [placed("v_codes%d" % a, [P, S], U32, v_codes_at[a]) for a in range(PASSES1)]
+        gain_skip = placed("gain_skip", [P, PASSES2, PACK], F32, v_codes_at[2])
 
-        w1_sc_raw = keep.tile([P, H], U8, name="w1_sc_raw", align_bytes=64)
-        rows_both = keep.tile([P, H + S], U8, name="rows_both", align_bytes=64)
-        gain_t = shared.tile([P, PASSES2, PACK], F32, name="gain_t", offset=66 * 1024, align_bytes=64)
-        skip_t = shared.tile([P, PASSES2, PACK], F32, name="skip_t", offset=66 * 1024 + 64, align_bytes=64)
-        mend_t = shared.tile([P, PASSES2, PACK], F32, name="mend_t", offset=66 * 1024 + 128, align_bytes=64)
-        planes = keep.tile([P, PASSES1 * (H + S)], U8, name="planes", align_bytes=64)
+        w1_sc_raw = keep.tile([P, H], U8, name="w1_sc_raw", align_bytes=ALIGN)
+        rows_both = placed("rows_both", [P, H + S], U8, rows_at)
+        gain_dealt = placed("gain_dealt", [P, PASSES2, PACK], F32, rows_at)
+        skip_dealt = placed("skip_dealt", [P, PASSES2, PACK], F32, rows_at + ALIGN)
+        mend_dealt = placed("mend_dealt", [P, PASSES2, PACK], F32, rows_at + 2 * ALIGN)
+        planes = keep.tile([P, PASSES1 * (H + S)], U8, name="planes", align_bytes=ALIGN)
+
         nc.sync.dma_start(
             out=w1_raw[:].bitcast(I32).rearrange("p (a c) -> p a c", a=PASSES1),
             in_=w1_words.bitcast(I32).rearrange("a p c -> p a c"),
@@ -76,8 +95,8 @@ def tile_list_plate_scratch_restorer_kernel(
             nc.sync.dma_start(
                 out=rows[FIRST_ROW:P, :].bitcast(I32), in_=scales.bitcast(I32).rearrange("a q c -> q a c")
             )
-            nc.vector.memset(rows[0:64, :].bitcast(I32), 0)
-            nc.vector.memset(rows[64:FIRST_ROW, :].bitcast(I32), 0)
+            nc.vector.memset(rows[0 : P // 2, :].bitcast(I32), 0)
+            nc.vector.memset(rows[P // 2 : FIRST_ROW, :].bitcast(I32), 0)
         nc.vector.memset(planes[:].bitcast(I32), 0)
 
         def load_tab(a):
@@ -87,21 +106,24 @@ def tile_list_plate_scratch_restorer_kernel(
 
         load_tab(0)
         load_tab(1)
+
         nc.vector.tensor_copy(
-            out=rows_both[:, :H].rearrange("p (g t q) -> p g t q", t=PACK, q=P),
-            in_=w1_sc_raw[:].rearrange("p (g q t) -> p g t q", t=PACK, q=P),
+            out=rows_both[:, :H].rearrange("p (b t m) -> p b t m", t=PACK, m=P),
+            in_=w1_sc_raw[:].rearrange("p (b m t) -> p b t m", t=PACK, m=P),
         )
         nc.vector.tensor_copy(out=v_sc_rows[:], in_=tab_sc[:].indirect(idx[:]))
         nc.vector.tensor_copy(out=rows_both[:, H:].bitcast(I32), in_=v_sc_rows[:].bitcast(I32))
-        for q in range(4):
-            first = FIRST_ROW + 4 * PASSES1 * q
-            (nc.scalar, nc.sync)[q % 2].dma_start(
-                out=planes[32 * q : 32 * q + 4, :].bitcast(I32).rearrange("r (a c) -> r a c", a=PASSES1),
-                in_=rows_both[first : first + 4 * PASSES1, :].bitcast(I32),
+        for quad in range(QUADRANTS):
+            first = FIRST_ROW + PLANE_ROWS * PASSES1 * quad
+            (nc.scalar, nc.sync)[quad % 2].dma_start(
+                out=planes[QUADRANT * quad : QUADRANT * quad + PLANE_ROWS, :]
+                .bitcast(I32)
+                .rearrange("r (a c) -> r a c", a=PASSES1),
+                in_=rows_both[first : first + PLANE_ROWS * PASSES1, :].bitcast(I32),
             )
         load_tab(2)
-        for dst, src in ((gain_t, gain), (skip_t, skip), (mend_t, mend)):
-            nc.scalar.dma_start(out=dst[:], in_=src.rearrange("(b p t) -> p b t", p=P, t=PACK))
+        for dealt, vector in ((gain_dealt, gain), (skip_dealt, skip), (mend_dealt, mend)):
+            nc.scalar.dma_start(out=dealt[:], in_=vector.rearrange("(b p t) -> p b t", p=P, t=PACK))
 
         fog_rows = fog.rearrange("(b p t) j -> b t p j", p=P, t=PACK)
         out_rows = out.rearrange("(b p t) j -> b t p j", p=P, t=PACK)
@@ -110,23 +132,21 @@ def tile_list_plate_scratch_restorer_kernel(
             nc.sync.dma_start(out=page[s][:], in_=fog_rows[s // PACK][s % PACK])
 
         def load_w2(b, c):
-            nc.sync.dma_start(
-                out=w2_raw[b, c][:],
-                in_=w2[b * K_PASS : (b + 1) * K_PASS, c * K_PASS : (c + 1) * K_PASS].rearrange("(p j) n -> p j n", j=PACK),
-            )
+            piece = w2[b * K_PASS : (b + 1) * K_PASS, c * K_PASS : (c + 1) * K_PASS]
+            nc.sync.dma_start(out=w2_raw[b, c][:], in_=piece.rearrange("(p i) n -> p i n", i=PACK))
 
         nc.vector.tensor_copy(
-            out=w1_codes[:].bitcast(U16).rearrange("p (g t q) -> p g t q", t=PACK, q=P),
-            in_=w1_raw[:].bitcast(U16).rearrange("p (g q t) -> p g t q", t=PACK, q=P),
+            out=w1_codes[:].bitcast(U16).rearrange("p (g t m) -> p g t m", t=PACK, m=P),
+            in_=w1_raw[:].bitcast(U16).rearrange("p (g m t) -> p g t m", t=PACK, m=P),
         )
 
-        cols = BANK // 16
+        list_cols = BANK // LIST_ROWS
 
         def gather_words(a):
             for h in range(HALVES):
                 nc.vector.tensor_copy(
                     out=v_codes[a][:, h * BANK : (h + 1) * BANK],
-                    in_=tab[a][:].indirect(idx[:, h * cols : (h + 1) * cols]),
+                    in_=tab[a][:].indirect(idx[:, h * list_cols : (h + 1) * list_cols]),
                 )
 
         gather_words(0)
@@ -138,10 +158,10 @@ def tile_list_plate_scratch_restorer_kernel(
         load_fog(3)
         load_w2(1, 0)
         gather_words(2)
-        for s in range(4, SLICES):
+        for s in range(PACK, SLICES):
             load_fog(s)
 
-        def first_pass(acc, s, h, a):
+        def first_product_pass(acc, s, h, a):
             col = a * H + s * P
             plane = a * (H + S)
             nc.tensor.matmul_mx(
@@ -155,20 +175,20 @@ def tile_list_plate_scratch_restorer_kernel(
             )
 
         feat = [keep.tile([P, S], F32, name="feat%d" % s) for s in range(SLICES)]
-        x_codes = [keep.tile([P, PICK], U32, name="x_codes%d" % b, align_bytes=64) for b in range(PASSES2)]
-        x_sc = [keep.tile([P, PICK], U8, name="x_sc%d" % b, align_bytes=64) for b in range(PASSES2)]
+        x_codes = [keep.tile([P, PICK], U32, name="x_codes%d" % b, align_bytes=ALIGN) for b in range(PASSES2)]
+        x_sc = [keep.tile([P, PICK], U8, name="x_sc%d" % b, align_bytes=ALIGN) for b in range(PASSES2)]
         w2_codes = {}
         w2_sc = {}
         for b in range(PASSES2):
-            for c in range(2):
-                w2_codes[b, c] = keep.tile([P, K_PASS], U32, name="w2_codes%d%d" % (b, c), align_bytes=64)
-                w2_sc[b, c] = keep.tile([P, K_PASS], U8, name="w2_sc%d%d" % (b, c), align_bytes=64)
+            for c in range(W2_HALVES):
+                w2_codes[b, c] = keep.tile([P, K_PASS], U32, name="w2_codes%d%d" % (b, c), align_bytes=ALIGN)
+                w2_sc[b, c] = keep.tile([P, K_PASS], U8, name="w2_sc%d%d" % (b, c), align_bytes=ALIGN)
 
         def quantise_w2(b, c):
-            grouped = ring.tile([P, PACK * K_PASS], BF16, name="w2_grouped", bufs=2, align_bytes=64)
+            grouped = ring.tile([P, PACK * K_PASS], BF16, name="w2_grouped", bufs=2, align_bytes=ALIGN)
             nc.scalar.copy(
-                out=grouped[:].rearrange("p (t q j) -> p q t j", t=PACK, j=PACK),
-                in_=w2_raw[b, c][:].rearrange("p j (q t) -> p q t j", t=PACK),
+                out=grouped[:].rearrange("p (t m i) -> p m t i", t=PACK, i=PACK),
+                in_=w2_raw[b, c][:].rearrange("p i (m t) -> p m t i", t=PACK),
             )
             nc.vector.quantize_mx(out=w2_codes[b, c][:].bitcast(FP8X4), scales=w2_sc[b, c][:], in_=grouped[:])
 
@@ -180,7 +200,7 @@ def tile_list_plate_scratch_restorer_kernel(
         for a in range(PASSES1):
             for h in range(HALVES):
                 for s in range(early):
-                    first_pass(accs[s, h], s, h, a)
+                    first_product_pass(accs[s, h], s, h, a)
 
         rounded = [ring.tile([P, PACK, PICK], BF16, name="rounded%d" % b, bufs=1) for b in range(PASSES2)]
 
@@ -189,7 +209,7 @@ def tile_list_plate_scratch_restorer_kernel(
                 if s >= early:
                     accs[s, h] = psum.tile([P, BANK], F32, name="acc", tag="acc")
                     for a in range(PASSES1):
-                        first_pass(accs[s, h], s, h, a)
+                        first_product_pass(accs[s, h], s, h, a)
                 half = slice(h * BANK, (h + 1) * BANK)
                 nc.vector.tensor_tensor(out=feat[s][:, half], in0=accs[s, h][:], in1=page[s][:, half], op=ADD)
             nc.scalar.activation(out=feat[s][:], in_=feat[s][:], func=TANH)
@@ -198,42 +218,48 @@ def tile_list_plate_scratch_restorer_kernel(
             b, t = divmod(s, PACK)
             picked = ring.tile([P, PICK], F32, name="picked")
             nc.vector.tensor_copy(out=picked[:], in_=feat[s][:].indirect(picks[:]))
-            nc.scalar.activation(out=rounded[b][:, t, :], in_=picked[:], func=COPY, scale=gain_t[:, b, t : t + 1])
+            nc.scalar.activation(out=rounded[b][:, t, :], in_=picked[:], func=COPY, scale=gain_dealt[:, b, t : t + 1])
 
-        def quantise_x(b):
-            woven = ring.tile([P, PICK * PACK], BF16, name="woven", bufs=2, align_bytes=64)
-            nc.vector.tensor_copy(
-                out=woven[:].rearrange("p (c i t) -> p c t i", i=4, t=PACK),
-                in_=rounded[b][:].rearrange("p t (c i) -> p c t i", i=4),
+        def quantise_x(b, weave):
+            woven = ring.tile([P, PICK * PACK], BF16, name="woven", bufs=PASSES2, align_bytes=ALIGN)
+            weave(
+                out=woven[:].rearrange("p (run e t) -> p run t e", e=4, t=PACK),
+                in_=rounded[b][:].rearrange("p t (run e) -> p run t e", e=4),
             )
             nc.vector.quantize_mx(out=x_codes[b][:].bitcast(FP8X4), scales=x_sc[b][:], in_=woven[:])
 
+        def prepare_first_piece():
+            quantise_w2(0, 0)
+            for quad in range(QUADRANTS):
+                nc.sync.dma_start(
+                    out=wgo_dealt[QUADRANT * quad : QUADRANT * (quad + 1), :],
+                    in_=wgo.rearrange("(q t) m -> q (t m)", t=PACK),
+                )
+
+        def prepare_second_piece():
+            quantise_w2(1, 0)
+            load_w2(0, 1)
+
+        after_pick = {
+            2: prepare_first_piece,
+            5: prepare_second_piece,
+            SLICES - 2: lambda: quantise_x(0, nc.scalar.copy),
+        }
         features(0)
         for s in range(SLICES):
             if s + 1 < SLICES:
                 features(s + 1)
             pick(s)
-            if s == 2:
-                quantise_w2(0, 0)
-                for u in range(4):
-                    nc.sync.dma_start(
-                        out=wgo_t[32 * u : 32 * u + 32, :], in_=wgo.rearrange("(q t) m -> q (t m)", t=PACK)
-                    )
-            if s == 4:
-                quantise_x(0)
-            if s == 5:
-                quantise_w2(1, 0)
-                load_w2(0, 1)
-        quantise_x(1)
+            if s in after_pick:
+                after_pick[s]()
+        quantise_x(1, nc.vector.tensor_copy)
         load_w2(1, 1)
-        nc.vector.tensor_tensor(out=gs_t[:], in0=gain_t[:], in1=skip_t[:], op=MULT)
+        nc.vector.tensor_tensor(out=gain_skip[:], in0=gain_dealt[:], in1=skip_dealt[:], op=MULT)
 
         for s in range(SLICES):
             c, t = divmod(s, PACK)
-            if s == 1:
-                quantise_w2(0, 1)
-            if s == 2:
-                quantise_w2(1, 1)
+            if 1 <= s <= PASSES2:
+                quantise_w2(s - 1, 1)
             acc = psum.tile([P, PICK], F32, name="acc", tag="acc")
             for b in range(PASSES2):
                 nc.tensor.matmul_mx(
@@ -247,12 +273,12 @@ def tile_list_plate_scratch_restorer_kernel(
                 )
             weight = ring.tile([P, PICK], F32, name="weight")
             nc.scalar.activation(
-                out=weight[:], in_=wgo_t[:, t * PICK : (t + 1) * PICK], func=COPY, scale=mend_t[:, c, t : t + 1]
+                out=weight[:], in_=wgo_dealt[:, t * PICK : (t + 1) * PICK], func=COPY, scale=mend_dealt[:, c, t : t + 1]
             )
             mended = ring.tile([P, PICK], F32, name="mended")
             nc.scalar.activation(out=mended[:], in_=acc[:], func=TANH)
             nc.vector.scalar_tensor_tensor(
-                out=page[s][:], in0=feat[s][:], scalar=gs_t[:, c, t : t + 1], in1=page[s][:], op0=MULT, op1=ADD
+                out=page[s][:], in0=feat[s][:], scalar=gain_skip[:, c, t : t + 1], in1=page[s][:], op0=MULT, op1=ADD
             )
             nc.vector.tensor_tensor(out=page[s][:].indirect(picks[:]), in0=mended[:], in1=weight[:], op=MULT)
             nc.sync.dma_start(out=out_rows[c][t], in_=page[s][:])

from contextlib import ExitStack

import concourse.mybir as mybir

K, T, S, H, PICK = 1536, 4096, 1024, 1024, 512
FLOPS = 2 * K * H * S + 2 * H * H * PICK

F32 = mybir.dt.float32
BF16 = mybir.dt.bfloat16
I32 = mybir.dt.int32
U32 = mybir.dt.uint32
U16 = mybir.dt.uint16
U8 = mybir.dt.uint8
FP8X4 = mybir.dt.float8_e4m3fn_x4
FP4X4 = mybir.dt.float4_e2m1fn_x4
MULT = mybir.AluOpType.mult
ADD = mybir.AluOpType.add
TANH = mybir.ActivationFunctionType.Tanh
COPY = mybir.ActivationFunctionType.Copy

P = 128
PACK = 4
K_PASS = P * PACK
BANK = 512
BANKS = 8
QUADRANTS = 4
QUADRANT = P // QUADRANTS
PLANE_ROWS = 4
LIST_ROWS = 16
PASSES1 = K // K_PASS
PASSES2 = H // K_PASS
SLICES = H // P
HALVES = S // BANK
W2_HALVES = H // K_PASS
RING = 3

FIRST_ROW = P - QUADRANTS * PLANE_ROWS * PASSES1

TAB_BYTES = 4 * T
PAGE_BYTES = 4 * S
ALIGN = 64


def tile_list_plate_scratch_restorer_kernel(
    tc, tab_words, tab_scales, offs, pos1, w1_words, w1_scales, fog, gain, w2, mend, skip, wgo, out
):
    nc = tc.nc
    with ExitStack() as ctx:
        lists = ctx.enter_context(tc.tile_pool(name="lists", bufs=1))
        keep = ctx.enter_context(tc.tile_pool(name="keep", bufs=1))
        shared = ctx.enter_context(tc.tile_pool(name="shared", bufs=1))
        ring = ctx.enter_context(tc.tile_pool(name="ring", bufs=RING))
        psum = ctx.enter_context(tc.psum_pool(name="psum", bufs=BANKS))

        idx = lists.tile([P, S // LIST_ROWS], U16, name="idx")
        picks = lists.tile([P, PICK // LIST_ROWS], U16, name="picks")
        nc.sync.dma_start(idx[:], offs)
        nc.sync.dma_start(picks[:], pos1)

        tab_at = [a * TAB_BYTES for a in range(PASSES1)]
        page_at = [tab_at[a] + i * PAGE_BYTES for a, count in enumerate((2, 2, 4)) for i in range(count)]
        piece_at = [tab_at[a] + 2 * PAGE_BYTES for a in range(PASSES2)]
        w1_codes_at = PASSES1 * TAB_BYTES
        v_codes_at = [w1_codes_at + PASSES1 * 2 * H + a * PAGE_BYTES for a in range(PASSES1)]
        rows_at = v_codes_at[-1] + PAGE_BYTES

        def placed(name, shape, dtype, at):
            return shared.tile(shape, dtype, name=name, offset=at, align_bytes=ALIGN)

        tab = [placed("tab%d" % a, [P, T], U32, tab_at[a]) for a in range(PASSES1)]
        tab_sc = placed("tab_sc", [P, T], U8, v_codes_at[1])
        w1_codes = placed("w1_codes", [P, PASSES1 * 2 * H], U8, w1_codes_at)
        w1_raw = keep.tile([P, PASSES1 * 2 * H], U8, name="w1_raw", align_bytes=ALIGN)
        v_sc_rows = placed("v_sc_rows", [P, S], U8, w1_codes_at - S // 2)
        page = [placed("page%d" % s, [P, S], F32, page_at[s]) for s in range(SLICES)]
        w2_raw = {}
        for b, c, at in ((0, 0, piece_at[0]), (1, 0, piece_at[1]), (0, 1, piece_at[1]), (1, 1, v_codes_at[0])):
            w2_raw[b, c] = placed("w2_raw%d%d" % (b, c), [P, PACK, K_PASS], F32, at)
        wgo_dealt = placed("wgo_dealt", [P, PACK * PICK], F32, piece_at[0])
        v_codes = [placed("v_codes%d" % a, [P, S], U32, v_codes_at[a]) for a in range(PASSES1)]
        gain_skip = placed("gain_skip", [P, PASSES2, PACK], F32, v_codes_at[2])

        w1_sc_raw = keep.tile([P, H], U8, name="w1_sc_raw", align_bytes=ALIGN)
        rows_both = placed("rows_both", [P, H + S], U8, rows_at)
        gain_dealt = placed("gain_dealt", [P, PASSES2, PACK], F32, rows_at)
        skip_dealt = placed("skip_dealt", [P, PASSES2, PACK], F32, rows_at + ALIGN)
        mend_dealt = placed("mend_dealt", [P, PASSES2, PACK], F32, rows_at + 2 * ALIGN)
        planes = keep.tile([P, PASSES1 * (H + S)], U8, name="planes", align_bytes=ALIGN)

        nc.sync.dma_start(
            out=w1_raw[:].bitcast(I32).rearrange("p (a c) -> p a c", a=PASSES1),
            in_=w1_words.bitcast(I32).rearrange("a p c -> p a c"),
        )
        for rows, scales in ((w1_sc_raw, w1_scales), (tab_sc, tab_scales)):
            nc.sync.dma_start(
                out=rows[FIRST_ROW:P, :].bitcast(I32), in_=scales.bitcast(I32).rearrange("a q c -> q a c")
            )
            nc.vector.memset(rows[0 : P // 2, :].bitcast(I32), 0)
            nc.vector.memset(rows[P // 2 : FIRST_ROW, :].bitcast(I32), 0)
        nc.vector.memset(planes[:].bitcast(I32), 0)

        def load_tab(a):
            nc.sync.dma_start(
                out=tab[a][:].bitcast(I32), in_=tab_words[a].rearrange("p t i -> p (t i)").bitcast(I32)
            )

        load_tab(0)
        load_tab(1)

        nc.vector.tensor_copy(
            out=rows_both[:, :H].rearrange("p (b t m) -> p b t m", t=PACK, m=P),
            in_=w1_sc_raw[:].rearrange("p (b m t) -> p b t m", t=PACK, m=P),
        )
        nc.vector.tensor_copy(out=v_sc_rows[:], in_=tab_sc[:].indirect(idx[:]))
        nc.vector.tensor_copy(out=rows_both[:, H:].bitcast(I32), in_=v_sc_rows[:].bitcast(I32))
        for quad in range(QUADRANTS):
            first = FIRST_ROW + PLANE_ROWS * PASSES1 * quad
            (nc.scalar, nc.sync)[quad % 2].dma_start(
                out=planes[QUADRANT * quad : QUADRANT * quad + PLANE_ROWS, :]
                .bitcast(I32)
                .rearrange("r (a c) -> r a c", a=PASSES1),
                in_=rows_both[first : first + PLANE_ROWS * PASSES1, :].bitcast(I32),
            )
        load_tab(2)
        for dealt, vector in ((gain_dealt, gain), (skip_dealt, skip), (mend_dealt, mend)):
            nc.scalar.dma_start(out=dealt[:], in_=vector.rearrange("(b p t) -> p b t", p=P, t=PACK))

        fog_rows = fog.rearrange("(b p t) j -> b t p j", p=P, t=PACK)
        out_rows = out.rearrange("(b p t) j -> b t p j", p=P, t=PACK)

        def load_fog(s):
            nc.sync.dma_start(out=page[s][:], in_=fog_rows[s // PACK][s % PACK])

        def load_w2(b, c):
            piece = w2[b * K_PASS : (b + 1) * K_PASS, c * K_PASS : (c + 1) * K_PASS]
            nc.sync.dma_start(out=w2_raw[b, c][:], in_=piece.rearrange("(p i) n -> p i n", i=PACK))

        nc.vector.tensor_copy(
            out=w1_codes[:].bitcast(U16).rearrange("p (g t m) -> p g t m", t=PACK, m=P),
            in_=w1_raw[:].bitcast(U16).rearrange("p (g m t) -> p g t m", t=PACK, m=P),
        )

        list_cols = BANK // LIST_ROWS

        def gather_words(a):
            for h in range(HALVES):
                nc.vector.tensor_copy(
                    out=v_codes[a][:, h * BANK : (h + 1) * BANK],
                    in_=tab[a][:].indirect(idx[:, h * list_cols : (h + 1) * list_cols]),
                )

        gather_words(0)
        load_fog(0)
        load_fog(1)
        load_w2(0, 0)
        gather_words(1)
        load_fog(2)
        load_fog(3)
        load_w2(1, 0)
        gather_words(2)
        for s in range(PACK, SLICES):
            load_fog(s)

        def first_product_pass(acc, s, h, a):
            col = a * H + s * P
            plane = a * (H + S)
            nc.tensor.matmul_mx(
                out=acc[:],
                lhsT=w1_codes[:, 2 * col : 2 * (col + P)].bitcast(FP4X4),
                lhsT_scale=planes[:, plane + s * P : plane + (s + 1) * P],
                rhs=v_codes[a][:, h * BANK : (h + 1) * BANK].bitcast(FP8X4),
                rhs_scale=planes[:, plane + H + h * BANK : plane + H + (h + 1) * BANK],
                start=(a == 0),
                stop=(a == PASSES1 - 1),
            )

        feat = [keep.tile([P, S], F32, name="feat%d" % s) for s in range(SLICES)]
        x_codes = [keep.tile([P, PICK], U32, name="x_codes%d" % b, align_bytes=ALIGN) for b in range(PASSES2)]
        x_sc = [keep.tile([P, PICK], U8, name="x_sc%d" % b, align_bytes=ALIGN) for b in range(PASSES2)]
        w2_codes = {}
        w2_sc = {}
        for b in range(PASSES2):
            for c in range(W2_HALVES):
                w2_codes[b, c] = keep.tile([P, K_PASS], U32, name="w2_codes%d%d" % (b, c), align_bytes=ALIGN)
                w2_sc[b, c] = keep.tile([P, K_PASS], U8, name="w2_sc%d%d" % (b, c), align_bytes=ALIGN)

        def quantise_w2(b, c):
            grouped = ring.tile([P, PACK * K_PASS], BF16, name="w2_grouped", bufs=2, align_bytes=ALIGN)
            nc.scalar.copy(
                out=grouped[:].rearrange("p (t m i) -> p m t i", t=PACK, i=PACK),
                in_=w2_raw[b, c][:].rearrange("p i (m t) -> p m t i", t=PACK),
            )
            nc.vector.quantize_mx(out=w2_codes[b, c][:].bitcast(FP8X4), scales=w2_sc[b, c][:], in_=grouped[:])

        early = BANKS // HALVES
        accs = {}
        for s in range(early):
            for h in range(HALVES):
                accs[s, h] = psum.tile([P, BANK], F32, name="acc", tag="acc")
        for a in range(PASSES1):
            for h in range(HALVES):
                for s in range(early):
                    first_product_pass(accs[s, h], s, h, a)

        rounded = [ring.tile([P, PACK, PICK], BF16, name="rounded%d" % b, bufs=1) for b in range(PASSES2)]

        def features(s):
            for h in range(HALVES):
                if s >= early:
                    accs[s, h] = psum.tile([P, BANK], F32, name="acc", tag="acc")
                    for a in range(PASSES1):
                        first_product_pass(accs[s, h], s, h, a)
                half = slice(h * BANK, (h + 1) * BANK)
                nc.vector.tensor_tensor(out=feat[s][:, half], in0=accs[s, h][:], in1=page[s][:, half], op=ADD)
            nc.scalar.activation(out=feat[s][:], in_=feat[s][:], func=TANH)

        def pick(s):
            b, t = divmod(s, PACK)
            picked = ring.tile([P, PICK], F32, name="picked")
            nc.vector.tensor_copy(out=picked[:], in_=feat[s][:].indirect(picks[:]))
            nc.scalar.activation(out=rounded[b][:, t, :], in_=picked[:], func=COPY, scale=gain_dealt[:, b, t : t + 1])

        def quantise_x(b, weave):
            woven = ring.tile([P, PICK * PACK], BF16, name="woven", bufs=PASSES2, align_bytes=ALIGN)
            weave(
                out=woven[:].rearrange("p (run e t) -> p run t e", e=4, t=PACK),
                in_=rounded[b][:].rearrange("p t (run e) -> p run t e", e=4),
            )
            nc.vector.quantize_mx(out=x_codes[b][:].bitcast(FP8X4), scales=x_sc[b][:], in_=woven[:])

        def prepare_first_piece():
            quantise_w2(0, 0)
            for quad in range(QUADRANTS):
                nc.sync.dma_start(
                    out=wgo_dealt[QUADRANT * quad : QUADRANT * (quad + 1), :],
                    in_=wgo.rearrange("(q t) m -> q (t m)", t=PACK),
                )

        def prepare_second_piece():
            quantise_w2(1, 0)
            load_w2(0, 1)

        after_pick = {
            2: prepare_first_piece,
            5: prepare_second_piece,
            SLICES - 2: lambda: quantise_x(0, nc.scalar.copy),
        }
        features(0)
        for s in range(SLICES):
            if s + 1 < SLICES:
                features(s + 1)
            pick(s)
            if s in after_pick:
                after_pick[s]()
        quantise_x(1, nc.vector.tensor_copy)
        load_w2(1, 1)
        nc.vector.tensor_tensor(out=gain_skip[:], in0=gain_dealt[:], in1=skip_dealt[:], op=MULT)

        for s in range(SLICES):
            c, t = divmod(s, PACK)
            if 1 <= s <= PASSES2:
                quantise_w2(s - 1, 1)
            acc = psum.tile([P, PICK], F32, name="acc", tag="acc")
            for b in range(PASSES2):
                nc.tensor.matmul_mx(
                    out=acc[:],
                    lhsT=w2_codes[b, c][:, t * P : (t + 1) * P].bitcast(FP8X4),
                    lhsT_scale=w2_sc[b, c][:, t * P : (t + 1) * P],
                    rhs=x_codes[b][:].bitcast(FP8X4),
                    rhs_scale=x_sc[b][:],
                    start=(b == 0),
                    stop=(b == PASSES2 - 1),
                )
            weight = ring.tile([P, PICK], F32, name="weight")
            nc.scalar.activation(
                out=weight[:], in_=wgo_dealt[:, t * PICK : (t + 1) * PICK], func=COPY, scale=mend_dealt[:, c, t : t + 1]
            )
            mended = ring.tile([P, PICK], F32, name="mended")
            nc.scalar.activation(out=mended[:], in_=acc[:], func=TANH)
            nc.vector.scalar_tensor_tensor(
                out=page[s][:], in0=feat[s][:], scalar=gain_skip[:, c, t : t + 1], in1=page[s][:], op0=MULT, op1=ADD
            )
            nc.vector.tensor_tensor(out=page[s][:].indirect(picks[:]), in0=mended[:], in1=weight[:], op=MULT)
            nc.sync.dma_start(out=out_rows[c][t], in_=page[s][:])
